import numpy as np
import ml_dtypes


def mxq(x, axis, fmt="e4m3"):
    dtype, down = {"e4m3": (ml_dtypes.float8_e4m3fn, 7), "e5m2": (ml_dtypes.float8_e5m2, 14)}[fmt]
    v = np.moveaxis(np.asarray(x, np.float32).astype(ml_dtypes.bfloat16).astype(np.float64), axis, -1)
    blocks = v.reshape(v.shape[:-1] + (-1, 32))
    amax = np.abs(blocks).max(-1, keepdims=True)
    byte = np.maximum(np.where(amax > 0, np.frexp(amax)[1] - 1 + 127, 0) - down, 1)
    scale = np.exp2(byte - 127.0)
    codes = (blocks / scale).astype(np.float32).astype(dtype).astype(np.float64)
    return np.moveaxis((codes * scale).reshape(v.shape), -1, axis)


WIDE = False


def mx_kscale(k):
    if not WIDE:
        return np.ones(k)
    levels = np.array([10, -10, 5, -5, 0])
    if k % 512:
        return np.exp2(np.random.permutation(np.resize(levels, k // 32))).repeat(32)
    a = np.empty((k // 512, 16))
    for p in range(k // 512):
        a[p, :8] = np.random.permutation(np.resize(levels, 8))
        for g in range(8):
            far = levels[np.abs(levels - a[p, g]) >= 10]
            a[p, g + 8] = far[np.random.randint(len(far))]
    return np.exp2(a.ravel()).repeat(32)


def f64(x):
    return np.asarray(x).astype(np.float64)


def striped(idx):
    return np.tile(idx.reshape(-1, 16).T, (8, 1)).astype(np.uint16)


def unstriped(offs):
    return offs[:16].T.reshape(-1).astype(np.int64)


E2M1 = np.array([0.0, 0.5, 1.0, 1.5, 2.0, 3.0, 4.0, 6.0, -0.0, -0.5, -1.0, -1.5, -2.0, -3.0, -4.0, -6.0])


def pack_weight(w, fmt):
    k, n = w.shape
    w = f64(np.asarray(w, np.float32).astype(ml_dtypes.bfloat16)).reshape(k // 32, 32, n)
    amax = np.abs(w).max(1)
    if fmt == "e4m3":
        byte = np.frexp(amax)[1] - 1 + 127 - 7
    else:
        mant, ex = np.frexp(amax / 6.0)
        byte = np.where(mant > 0.5, ex, ex - 1) + 127
    byte = np.clip(np.where(amax > 0, byte, 1), 1, 254)
    scaled = (w * np.exp2(127.0 - byte)[:, None, :]).reshape(k, n).astype(np.float32)
    by_word = np.ascontiguousarray(scaled.reshape(k // 512, 128, 4, n).transpose(0, 1, 3, 2))
    if fmt == "e4m3":
        words = by_word.astype(ml_dtypes.float8_e4m3fn).view(np.uint8)
    else:
        c = by_word.astype(ml_dtypes.float4_e2m1fn).view(np.uint8) & 0xF
        words = (c[..., 0::2] | (c[..., 1::2] << 4)).reshape(k // 512, 128, 2 * n)
    return np.ascontiguousarray(words), np.ascontiguousarray(byte.astype(np.uint8).reshape(k // 512, 16, n))


def unpack_weight(words, scales, fmt):
    g, _, n = scales.shape
    words = np.ascontiguousarray(words).reshape(g, 128, n, -1)
    if fmt == "e4m3":
        vals = words.view(ml_dtypes.float8_e4m3fn).astype(np.float64)
    else:
        nib = np.empty((g, 128, n, 4), np.uint8)
        nib[..., 0::2] = words & 0xF
        nib[..., 1::2] = words >> 4
        vals = E2M1[nib]
    vals = vals * np.repeat(np.exp2(scales.astype(np.float64) - 127.0), 8, axis=1)[..., None]
    return vals.transpose(0, 1, 3, 2).reshape(g * 512, n)


def gelu(v):
    return 0.5 * v * (1.0 + np.tanh(np.sqrt(2.0 / np.pi) * (v + 0.044715 * v**3)))


def striped8(idx):
    return np.concatenate([v.reshape(-1, 16).T for v in idx]).astype(np.uint16)


def unstriped8(offs):
    return np.stack([offs[16 * g:16 * g + 16].T.reshape(-1) for g in range(8)]).astype(np.int64)


def heads(h, wgt, idx8):
    r = np.arange(h.shape[0])
    return wgt[r // 4 % 128] * h[r[:, None], idx8[r % 512 // 64]]


def put_heads(h, wgs, idx8, t2):
    r = np.arange(h.shape[0])
    page = np.zeros((h.shape[0], t2))
    page[r[:, None], idx8[r % 512 // 64]] = wgs[r // 4 % 128] * h
    return page


K, H, N, T, S, P, T2 = 1024, 1024, 512, 2048, 1024, 1024, 2048

def setup_inputs():
    n = np.random.standard_normal
    s = mx_kscale(K)[:, None]
    u = mx_kscale(H)[:, None]
    d = {}
    d["tab_words"], d["tab_scales"] = pack_weight(n((K, T)) * s, "e4m3")
    d["offs"] = striped(np.random.permutation(T)[:S])
    d["offs2"] = striped8(np.stack([np.random.permutation(T2)[:S] for _ in range(8)]))
    d["offs3"] = striped8(np.stack([np.random.permutation(T2)[:P] for _ in range(8)]))
    d["w1"] = (n((K, H)) / s * u.T / K**0.5).astype(np.float32)
    d["w2_words"], d["w2_scales"] = pack_weight(n((K, H)) / s * u.T / K**0.5, "e2m1")
    d["thr"] = (0.8 * n(H) * u[:, 0]).astype(np.float32)
    d["wgs"] = np.repeat(np.random.uniform(0.5, 2.0, (8, S)), 16, axis=0).astype(np.float32)
    d["wgt"] = np.repeat(np.random.uniform(0.5, 2.0, (8, P)), 16, axis=0).astype(np.float32)
    d["bark"] = (n((H, P)) * u).astype(np.float32)
    d["w3"] = (0.6 * n((H, N)) / u / H**0.5).astype(np.float32)
    d["pan"] = (1.5 * np.exp(0.3 * n(N))).astype(np.float32)
    return d

def reference(tab_words, tab_scales, offs, offs2, offs3, w1, w2_words, w2_scales, thr, wgs, wgt, bark, w3, pan):
    v = unpack_weight(tab_words, tab_scales, "e4m3")[:, unstriped(offs)]
    w2 = unpack_weight(w2_words, w2_scales, "e2m1")
    a = mxq(f64(w1), 0, "e4m3").T @ v
    b = w2.T @ v
    h = a - np.abs(b - f64(thr)[:, None])
    page = put_heads(h, f64(wgs), unstriped8(offs2), T2)
    x = heads(page, f64(wgt), unstriped8(offs3))
    z = x + f64(bark)
    y = mxq(f64(w3), 0, "e4m3").T @ mxq(z, 0, "e4m3")
    return y + f64(pan)[:, None] * np.tanh(y)

@@ -1,0 +1,333 @@
+from contextlib import ExitStack
+
+import concourse.mybir as mybir
+from concourse.masks import make_identity
+
+K, H, N, T, S, M, T2 = 1024, 1024, 512, 2048, 1024, 1024, 2048
+FLOPS = 2 * (2 * K * H * S + H * N * M)
+
+F32 = mybir.dt.float32
+BF16 = mybir.dt.bfloat16
+I32 = mybir.dt.int32
+U32 = mybir.dt.uint32
+U16 = mybir.dt.uint16
+U8 = mybir.dt.uint8
+FP8X4 = mybir.dt.float8_e4m3fn_x4
+FP4X4 = mybir.dt.float4_e2m1fn_x4
+ALU = mybir.AluOpType
+ACT = mybir.ActivationFunctionType
+
+P = 128
+BANK = 512
+CHUNK = 256
+PAGES = 2
+Y_CHUNKS = ((0, 512), (512, 256), (768, 256))
+
+
+def tile_list_cork_taint_scores_kernel(
+    tc, tab_words, tab_scales, offs, offs2, offs3, w1, w2_words, w2_scales, thr, wgs, wgt, bark, w3, pan, out
+):
+    nc = tc.nc
+    with ExitStack() as ctx:
+        keep = ctx.enter_context(tc.tile_pool(name="keep", bufs=1))
+        ring = ctx.enter_context(tc.tile_pool(name="ring", bufs=2))
+        psum = ctx.enter_context(tc.psum_pool(name="psum", bufs=4))
+
+        def kept(shape, dtype, name):
+            return keep.tile(shape, dtype, name=name, align_bytes=64)
+
+        def ringed(shape, dtype, tag, bufs):
+            return ring.tile(shape, dtype, name=tag, tag=tag, bufs=bufs, align_bytes=64)
+
+        list1 = keep.tile([P, S // 16], U16, name="list1")
+        list2 = keep.tile([P, S // 16], U16, name="list2")
+        list3 = keep.tile([P, M // 16], U16, name="list3")
+        tab_s = kept([P, T], U8, "tab_s")
+        w2_s_raw = kept([P, 2, H], U8, "w2_s_raw")
+        picked_s = kept([P, S], U8, "picked_s")
+        picked_s1 = kept([P, S], U8, "picked_s1")
+        pages = [kept([P, T2], F32, "page%d" % g) for g in range(PAGES)]
+        thr_sb = kept([P, 2, 4], F32, "thr_sb")
+        pan_sb = kept([P, 4], F32, "pan_sb")
+        wgs_sb = kept([P, S], F32, "wgs_sb")
+        wgt_sb = kept([P, M], F32, "wgt_sb")
+        ident = kept([P, P], F32, "ident")
+        warm = kept([P, 8], F32, "warm")
+
+        nc.vector.memset(tab_s[:].bitcast(I32), 0)
+        nc.vector.memset(w2_s_raw[:].rearrange("p a c -> p (a c)").bitcast(I32), 0)
+        nc.vector.memset(picked_s1[:].bitcast(I32), 0)
+        nc.vector.memset(warm[:], 0.0)
+        nc.scalar.activation(out=warm[:, 4:5], in_=warm[:, 0:1], func=ACT.Tanh)
+        make_identity(nc, ident[:])
+
+        def load_w2_words(b):
+            raw = ringed([P, 2, 1024], U8, "w2_raw", 2)
+            nc.sync.dma_start(
+                raw[:].bitcast(I32),
+                w2_words[:, :, 1024 * b : 1024 * (b + 1)].rearrange("a p c -> p a c").bitcast(I32),
+            )
+            return raw
+
+        def load_rows(src):
+            raw = ringed([P, 4, BANK], F32, "w_raw", 3)
+            nc.sync.dma_start(raw[:], src.rearrange("(p j) c -> p j c", j=4))
+            return raw
+
+        w1_raw = {}
+        nc.sync.dma_start(list1[:], offs)
+        w1_raw[0, 0] = load_rows(w1[0:512, 0:512])
+        for q in range(4):
+            nc.sync.dma_start(
+                tab_s[32 * q : 32 * q + 8, :].bitcast(I32), tab_scales[:, 4 * q : 4 * q + 4, :].bitcast(I32)
+            )
+        w2_raw = [load_w2_words(0)]
+        for q in range(4):
+            nc.sync.dma_start(
+                w2_s_raw[32 * q : 32 * q + 4, :, :].bitcast(I32),
+                w2_scales[:, 4 * q : 4 * q + 4, :].rearrange("a r c -> r a c").bitcast(I32),
+            )
+        w1_raw[1, 0] = load_rows(w1[512:1024, 0:512])
+        tab_w = []
+        for a in range(2):
+            words = ringed([P, T], I32, "big", 2)
+            nc.sync.dma_start(words[:], tab_words[a].rearrange("p t i -> p (t i)").bitcast(I32))
+            tab_w.append(words)
+        for g in range(PAGES):
+            nc.vector.memset(pages[g][:], 0.0)
+        nc.sync.dma_start(thr_sb[:], thr.rearrange("(b p i) -> p b i", b=2, i=4))
+        nc.sync.dma_start(list2[:], offs2)
+        nc.sync.dma_start(wgs_sb[:], wgs)
+        nc.sync.dma_start(list3[:], offs3)
+        nc.sync.dma_start(wgt_sb[:], wgt)
+
+        nc.vector.tensor_copy(picked_s[:], tab_s[:].indirect(list1[:]))
+        for q in range(4):
+            nc.scalar.dma_start(
+                picked_s1[32 * q : 32 * q + 4, :].bitcast(I32), picked_s[32 * q + 4 : 32 * q + 8, :].bitcast(I32)
+            )
+        picked_w = {}
+
+        def pick_words(a, half):
+            words = kept([P, BANK], U32, "picked_w%d%d" % (a, half))
+            nc.vector.tensor_copy(words[:], tab_w[a][:].bitcast(U32).indirect(list1[:, 32 * half : 32 * (half + 1)]))
+            picked_w[a, half] = words
+
+        def deal_w2(b):
+            words = kept([P, 2, 1024], U8, "w2_w%d" % b)
+            scales = kept([P, 2, BANK], U8, "w2_s%d" % b)
+            nc.vector.tensor_copy(
+                words[:].bitcast(U16).rearrange("p a (i q) -> p a i q", i=4),
+                w2_raw[b][:].bitcast(U16).rearrange("p a (q i) -> p a i q", i=4),
+            )
+            nc.vector.tensor_copy(
+                scales[:].rearrange("p a (i q) -> p a i q", i=4),
+                w2_s_raw[:, :, 512 * b : 512 * (b + 1)].rearrange("p a (q i) -> p a i q", i=4),
+            )
+            return words, scales
+
+        def round_rows(raw, copy):
+            grouped = ringed([P, 4 * BANK], BF16, "w_bf", 3)
+            copy(
+                grouped[:].rearrange("p (i q j) -> p q i j", i=4, j=4),
+                raw[:].rearrange("p j (q i) -> p q i j", i=4),
+            )
+            return grouped
+
+        def quantize_rows(grouped, name):
+            codes = kept([P, BANK], U32, name + "_c")
+            scales = kept([P, BANK], U8, name + "_s")
+            nc.vector.quantize_mx(out=codes[:].bitcast(FP8X4), scales=scales[:], in_=grouped[:])
+            return codes, scales
+
+        w2_q = [deal_w2(0)]
+        w1_q = {}
+        w1_q[0, 0] = quantize_rows(round_rows(w1_raw[0, 0], nc.scalar.copy), "w1_00")
+        pick_words(0, 0)
+        w1_q[1, 0] = quantize_rows(round_rows(w1_raw[1, 0], nc.scalar.copy), "w1_10")
+        pick_words(1, 0)
+        pick_words(0, 1)
+        pick_words(1, 1)
+
+        bark_sb = {}
+
+        def load_bark(b, u):
+            rows = ringed([P, 2, M], F32, "bark", 2)
+            nc.sync.dma_start(
+                rows[:], bark[512 * b : 512 * (b + 1), :].rearrange("(p i) m -> p i m", i=4)[:, 2 * u : 2 * u + 2, :]
+            )
+            bark_sb[b, u] = rows
+
+        load_bark(0, 0)
+        for a in range(2):
+            w1_raw[a, 1] = load_rows(w1[512 * a : 512 * (a + 1), 512:1024])
+        w2_raw.append(load_w2_words(1))
+        load_bark(0, 1)
+        w3_raw = [load_rows(w3[512 * b : 512 * (b + 1), :]) for b in range(2)]
+        nc.sync.dma_start(pan_sb[:], pan.rearrange("(p t) -> p t", t=4))
+
+        h_sb = {}
+        x_sb = {}
+
+        def features(s, half):
+            b, i = divmod(s, 4)
+            cols = slice(BANK * half, BANK * (half + 1))
+            rows = slice(P * i, P * (i + 1))
+            if half == 0:
+                h_sb[s] = ringed([P, S], F32, "h", 3)
+            b_ps = psum.tile([P, BANK], F32, name="mx", tag="mx")
+            a_ps = psum.tile([P, BANK], F32, name="mx", tag="mx")
+            w2_w, w2_s = w2_q[b]
+            for a in range(2):
+                nc.tensor.matmul_mx(
+                    out=b_ps[:],
+                    lhsT=w2_w[:, a, 2 * P * i : 2 * P * (i + 1)].bitcast(FP4X4),
+                    lhsT_scale=w2_s[:, a, rows],
+                    rhs=picked_w[a, half][:].bitcast(FP8X4),
+                    rhs_scale=(picked_s, picked_s1)[a][:, cols],
+                    start=(a == 0),
+                    stop=(a == 1),
+                )
+                codes, scales = w1_q[a, b]
+                nc.tensor.matmul_mx(
+                    out=a_ps[:],
+                    lhsT=codes[:, rows].bitcast(FP8X4),
+                    lhsT_scale=scales[:, rows],
+                    rhs=picked_w[a, half][:].bitcast(FP8X4),
+                    rhs_scale=(picked_s, picked_s1)[a][:, cols],
+                    start=(a == 0),
+                    stop=(a == 1),
+                )
+            dist = ringed([P, BANK], F32, "dist", 4)
+            nc.scalar.activation(out=dist[:], in_=b_ps[:], func=ACT.Abs, bias=thr_sb[:, b, i : i + 1], scale=-1.0)
+            nc.vector.tensor_tensor(h_sb[s][:, cols], a_ps[:], dist[:], ALU.subtract)
+
+        def put(s, lo, hi):
+            nc.vector.tensor_tensor(
+                pages[s % PAGES][:].indirect(list2[:, lo // 16 : hi // 16]),
+                h_sb[s][:, lo:hi],
+                wgs_sb[:, lo:hi],
+                ALU.mult,
+            )
+
+        def pick(s, lo, hi):
+            if lo == 0:
+                x_sb[s] = ringed([P, M], F32, "x", 4)
+            nc.vector.tensor_tensor(
+                x_sb[s][:, lo:hi],
+                pages[s % PAGES][:].indirect(list3[:, lo // 16 : hi // 16]),
+                wgt_sb[:, lo:hi],
+                ALU.mult,
+            )
+
+        z_turned = {}
+        z_codes = [kept([P, M], U32, "z_c%d" % b) for b in range(2)]
+        z_scales = [kept([P, M], U8, "z_s%d" % b) for b in range(2)]
+
+        def add_bark(b, u, k):
+            bank = psum.tile([P, 2, 2, P], F32, name="tr", tag="tr")
+            for t in range(2):
+                cols = slice(CHUNK * k + P * t, CHUNK * k + P * (t + 1))
+                for e in range(2):
+                    nc.tensor.matmul(
+                        bank[:, t, e, :], bark_sb[b, u][:, e, cols], ident[:], start=True, stop=False, is_transpose=True
+                    )
+                    nc.tensor.matmul(
+                        bank[:, t, e, :],
+                        x_sb[4 * b + 2 * u + e][:, cols],
+                        ident[:],
+                        start=False,
+                        stop=True,
+                        is_transpose=True,
+                    )
+            turned = ringed([P, 2 * CHUNK], BF16, "z_turned", 8)
+            nc.scalar.copy(
+                turned[:].rearrange("m (t p e) -> m t p e", t=2, e=2), bank[:].rearrange("m t e p -> m t p e")
+            )
+            z_turned[b, u, k] = turned
+
+        def quantize_z(b, k):
+            bank = psum.tile([P, 2, 2, P], F32, name="tr", tag="tr")
+            for t in range(2):
+                for u in range(2):
+                    nc.tensor.transpose(
+                        bank[:, t, u, :], z_turned[b, u, k][:].bitcast(F32)[:, P * t : P * (t + 1)], ident[:]
+                    )
+            grouped = ringed([P, 4 * CHUNK], BF16, "z_bf", 4)
+            nc.scalar.copy(
+                grouped[:].bitcast(F32).rearrange("p (t m u) -> p t m u", t=2, u=2),
+                bank[:].rearrange("p t u m -> p t m u"),
+            )
+            cols = slice(CHUNK * k, CHUNK * (k + 1))
+            nc.vector.quantize_mx(out=z_codes[b][:, cols].bitcast(FP8X4), scales=z_scales[b][:, cols], in_=grouped[:])
+
+        out_rows = out.rearrange("(p t) m -> p t m", t=4)
+
+        def scores(lo, width):
+            cols = slice(lo, lo + width)
+            per_bank = BANK // width
+            for t0 in range(0, 4, per_bank):
+                y_ps = psum.tile([P, per_bank, width], F32, name="mx", tag="mx")
+                for t in range(per_bank):
+                    rows = slice(P * (t0 + t), P * (t0 + t + 1))
+                    for b in range(2):
+                        codes, scales = w3_q[b]
+                        nc.tensor.matmul_mx(
+                            out=y_ps[:, t, :],
+                            lhsT=codes[:, rows].bitcast(FP8X4),
+                            lhsT_scale=scales[:, rows],
+                            rhs=z_codes[b][:, cols].bitcast(FP8X4),
+                            rhs_scale=z_scales[b][:, cols],
+                            start=(b == 0),
+                            stop=(b == 1),
+                        )
+                bent = ringed([P, per_bank, width], F32, "bent", 4)
+                nc.scalar.activation(out=bent[:], in_=y_ps[:], func=ACT.Tanh)
+                result = ringed([P, per_bank, width], F32, "result", 4)
+                for t in range(per_bank):
+                    nc.vector.scalar_tensor_tensor(
+                        result[:, t, :],
+                        bent[:, t, :],
+                        pan_sb[:, t0 + t : t0 + t + 1],
+                        y_ps[:, t, :],
+                        ALU.mult,
+                        ALU.add,
+                    )
+                nc.sync.dma_start(out_rows[:, t0 : t0 + per_bank, cols], result[:])
+
+        w3_q = []
+        features(0, 0)
+        put(0, 0, BANK)
+        features(0, 1)
+        put(0, BANK, S)
+        for s in range(1, 8):
+            features(s, 0)
+            features(s, 1)
+            if s < 7:
+                pick(s - 1, 0, M)
+            if s == 1:
+                for a in range(2):
+                    w1_q[a, 1] = quantize_rows(round_rows(w1_raw[a, 1], nc.scalar.copy), "w1_%d1" % a)
+                w2_q.append(deal_w2(1))
+            if s == 4:
+                for b in range(2):
+                    w3_q.append(quantize_rows(round_rows(w3_raw[b], nc.scalar.copy), "w3_%d" % b))
+            put(s, 0, S)
+            if s % 2 == 0:
+                b, u = divmod(s // 2 - 1, 2)
+                for k in range(M // CHUNK):
+                    add_bark(b, u, k)
+                    if u == 1:
+                        quantize_z(b, k)
+                if s < 6:
+                    load_bark(1, u)
+        done = 0
+        for k in range(M // CHUNK):
+            pick(6, CHUNK * k, CHUNK * (k + 1))
+            pick(7, CHUNK * k, CHUNK * (k + 1))
+            add_bark(1, 1, k)
+            quantize_z(1, k)
+            lo, width = Y_CHUNKS[done]
+            if lo + width == CHUNK * (k + 1):
+                scores(lo, width)
+                done = done + 1

@@ -19,9 +19,9 @@ ACT = mybir.ActivationFunctionType
 
 P = 128
 BANK = 512
-CHUNK = 256
-PAGES = 2
-Y_CHUNKS = ((0, 512), (512, 256), (768, 256))
+PAGES = 3
+EVEN_CHUNKS = ((0, 256), (256, 256), (512, 256), (768, 256))
+LAST_CHUNKS = ((0, 128), (128, 256), (384, 256), (640, 256), (896, 128))
 
 
 def tile_list_cork_taint_scores_kernel(
@@ -42,10 +42,8 @@ def tile_list_cork_taint_scores_kernel(
         list1 = keep.tile([P, S // 16], U16, name="list1")
         list2 = keep.tile([P, S // 16], U16, name="list2")
         list3 = keep.tile([P, M // 16], U16, name="list3")
-        tab_s = kept([P, T], U8, "tab_s")
+        tab_s = kept([P, 2 * T], U8, "tab_s")
         w2_s_raw = kept([P, 2, H], U8, "w2_s_raw")
-        picked_s = kept([P, S], U8, "picked_s")
-        picked_s1 = kept([P, S], U8, "picked_s1")
         pages = [kept([P, T2], F32, "page%d" % g) for g in range(PAGES)]
         thr_sb = kept([P, 2, 4], F32, "thr_sb")
         pan_sb = kept([P, 4], F32, "pan_sb")
@@ -54,12 +52,10 @@ def tile_list_cork_taint_scores_kernel(
         ident = kept([P, P], F32, "ident")
         warm = kept([P, 8], F32, "warm")
 
-        nc.vector.memset(tab_s[:].bitcast(I32), 0)
-        nc.vector.memset(w2_s_raw[:].rearrange("p a c -> p (a c)").bitcast(I32), 0)
-        nc.vector.memset(picked_s1[:].bitcast(I32), 0)
+        nc.gpsimd.memset(tab_s[:].bitcast(I32), 0)
         nc.vector.memset(warm[:], 0.0)
+        nc.gpsimd.memset(w2_s_raw[:].rearrange("p a c -> p (a c)").bitcast(I32), 0)
         nc.scalar.activation(out=warm[:, 4:5], in_=warm[:, 0:1], func=ACT.Tanh)
-        make_identity(nc, ident[:])
 
         def load_w2_words(b):
             raw = ringed([P, 2, 1024], U8, "w2_raw", 2)
@@ -74,44 +70,45 @@ def tile_list_cork_taint_scores_kernel(
             nc.sync.dma_start(raw[:], src.rearrange("(p j) c -> p j c", j=4))
             return raw
 
+        def load_table_words(a):
+            words = ringed([P, T], I32, "big", 2)
+            nc.sync.dma_start(words[:], tab_words[a].rearrange("p t i -> p (t i)").bitcast(I32))
+            return words
+
         w1_raw = {}
         nc.sync.dma_start(list1[:], offs)
-        w1_raw[0, 0] = load_rows(w1[0:512, 0:512])
+        tab_w = [load_table_words(0)]
         for q in range(4):
             nc.sync.dma_start(
-                tab_s[32 * q : 32 * q + 8, :].bitcast(I32), tab_scales[:, 4 * q : 4 * q + 4, :].bitcast(I32)
+                tab_s[32 * q : 32 * q + 4, :].bitcast(I32).rearrange("r (a t) -> r a t", a=2),
+                tab_scales[:, 4 * q : 4 * q + 4, :].rearrange("a r t -> r a t").bitcast(I32),
             )
+        for a in range(2):
+            w1_raw[a, 0] = load_rows(w1[512 * a : 512 * (a + 1), 0:512])
         w2_raw = [load_w2_words(0)]
         for q in range(4):
             nc.sync.dma_start(
                 w2_s_raw[32 * q : 32 * q + 4, :, :].bitcast(I32),
                 w2_scales[:, 4 * q : 4 * q + 4, :].rearrange("a r c -> r a c").bitcast(I32),
             )
-        w1_raw[1, 0] = load_rows(w1[512:1024, 0:512])
-        tab_w = []
-        for a in range(2):
-            words = ringed([P, T], I32, "big", 2)
-            nc.sync.dma_start(words[:], tab_words[a].rearrange("p t i -> p (t i)").bitcast(I32))
-            tab_w.append(words)
+        tab_w.append(load_table_words(1))
         for g in range(PAGES):
-            nc.vector.memset(pages[g][:], 0.0)
+            (nc.vector, nc.vector, nc.gpsimd)[g].memset(pages[g][:].bitcast(I32), 0)
+        make_identity(nc, ident[:])
         nc.sync.dma_start(thr_sb[:], thr.rearrange("(b p i) -> p b i", b=2, i=4))
         nc.sync.dma_start(list2[:], offs2)
         nc.sync.dma_start(wgs_sb[:], wgs)
+        w2_raw.append(load_w2_words(1))
         nc.sync.dma_start(list3[:], offs3)
         nc.sync.dma_start(wgt_sb[:], wgt)
 
-        nc.vector.tensor_copy(picked_s[:], tab_s[:].indirect(list1[:]))
-        for q in range(4):
-            nc.scalar.dma_start(
-                picked_s1[32 * q : 32 * q + 4, :].bitcast(I32), picked_s[32 * q + 4 : 32 * q + 8, :].bitcast(I32)
-            )
-        picked_w = {}
+        picked_w = [kept([P, S], U32, "picked_w%d" % a) for a in range(2)]
+        picked_s = [kept([P, S], U8, "picked_s%d" % a) for a in range(2)]
 
-        def pick_words(a, half):
-            words = kept([P, BANK], U32, "picked_w%d%d" % (a, half))
-            nc.vector.tensor_copy(words[:], tab_w[a][:].bitcast(U32).indirect(list1[:, 32 * half : 32 * (half + 1)]))
-            picked_w[a, half] = words
+        def pick_words(a, lo, hi):
+            nc.vector.tensor_copy(
+                picked_w[a][:, lo:hi], tab_w[a][:].bitcast(U32).indirect(list1[:, lo // 16 : hi // 16])
+            )
 
         def deal_w2(b):
             words = kept([P, 2, 1024], U8, "w2_w%d" % b)
@@ -140,14 +137,15 @@ def tile_list_cork_taint_scores_kernel(
             nc.vector.quantize_mx(out=codes[:].bitcast(FP8X4), scales=scales[:], in_=grouped[:])
             return codes, scales
 
-        w2_q = [deal_w2(0)]
+        pick_words(0, 0, S)
+        for a in range(2):
+            nc.vector.tensor_copy(picked_s[a][:], tab_s[:, T * a : T * (a + 1)].indirect(list1[:]))
         w1_q = {}
         w1_q[0, 0] = quantize_rows(round_rows(w1_raw[0, 0], nc.scalar.copy), "w1_00")
-        pick_words(0, 0)
+        w2_q = [deal_w2(0)]
+        pick_words(1, 0, BANK)
         w1_q[1, 0] = quantize_rows(round_rows(w1_raw[1, 0], nc.scalar.copy), "w1_10")
-        pick_words(1, 0)
-        pick_words(0, 1)
-        pick_words(1, 1)
+        pick_words(1, BANK, S)
 
         bark_sb = {}
 
@@ -161,20 +159,21 @@ def tile_list_cork_taint_scores_kernel(
         load_bark(0, 0)
         for a in range(2):
             w1_raw[a, 1] = load_rows(w1[512 * a : 512 * (a + 1), 512:1024])
-        w2_raw.append(load_w2_words(1))
         load_bark(0, 1)
         w3_raw = [load_rows(w3[512 * b : 512 * (b + 1), :]) for b in range(2)]
         nc.sync.dma_start(pan_sb[:], pan.rearrange("(p t) -> p t", t=4))
 
         h_sb = {}
         x_sb = {}
+        terms = {}
+        h_turned = {}
 
         def features(s, half):
             b, i = divmod(s, 4)
             cols = slice(BANK * half, BANK * (half + 1))
             rows = slice(P * i, P * (i + 1))
             if half == 0:
-                h_sb[s] = ringed([P, S], F32, "h", 3)
+                h_sb[s] = ringed([P, S], F32, "h", 3) if s < 7 else ringed([P, S], F32, "x2", 1)
             b_ps = psum.tile([P, BANK], F32, name="mx", tag="mx")
             a_ps = psum.tile([P, BANK], F32, name="mx", tag="mx")
             w2_w, w2_s = w2_q[b]
@@ -183,8 +182,8 @@ def tile_list_cork_taint_scores_kernel(
                     out=b_ps[:],
                     lhsT=w2_w[:, a, 2 * P * i : 2 * P * (i + 1)].bitcast(FP4X4),
                     lhsT_scale=w2_s[:, a, rows],
-                    rhs=picked_w[a, half][:].bitcast(FP8X4),
-                    rhs_scale=(picked_s, picked_s1)[a][:, cols],
+                    rhs=picked_w[a][:, cols].bitcast(FP8X4),
+                    rhs_scale=picked_s[a][:, cols],
                     start=(a == 0),
                     stop=(a == 1),
                 )
@@ -193,14 +192,54 @@ def tile_list_cork_taint_scores_kernel(
                     out=a_ps[:],
                     lhsT=codes[:, rows].bitcast(FP8X4),
                     lhsT_scale=scales[:, rows],
-                    rhs=picked_w[a, half][:].bitcast(FP8X4),
-                    rhs_scale=(picked_s, picked_s1)[a][:, cols],
+                    rhs=picked_w[a][:, cols].bitcast(FP8X4),
+                    rhs_scale=picked_s[a][:, cols],
                     start=(a == 0),
                     stop=(a == 1),
                 )
             dist = ringed([P, BANK], F32, "dist", 4)
             nc.scalar.activation(out=dist[:], in_=b_ps[:], func=ACT.Abs, bias=thr_sb[:, b, i : i + 1], scale=-1.0)
-            nc.vector.tensor_tensor(h_sb[s][:, cols], a_ps[:], dist[:], ALU.subtract)
+            if s == 0:
+                nc.vector.tensor_tensor(h_sb[s][:, cols], a_ps[:], dist[:], ALU.subtract)
+            else:
+                if half == 0 and s >= 2:
+                    minus_a = ringed([P, BANK], F32, "x%d" % ((s - 2) % 4), 1)
+                else:
+                    minus_a = ringed([P, BANK], F32, "minus_a", 2)
+                nc.scalar.activation(out=minus_a[:], in_=a_ps[:], func=ACT.Copy, scale=-1.0)
+                terms[s, half] = (dist, minus_a)
+
+        def add_terms(s, half):
+            bank = psum.tile([P, 4, P], F32, name="tr", tag="tr")
+            for t in range(4):
+                for n, term in enumerate(terms[s, half]):
+                    nc.tensor.matmul(
+                        bank[:, t, :],
+                        term[:, P * t : P * (t + 1)],
+                        ident[:],
+                        start=(n == 0),
+                        stop=(n == 1),
+                        is_transpose=True,
+                    )
+            turned = ringed([P, BANK], F32, "h_turned", 2)
+            nc.scalar.copy(turned[:], bank[:].rearrange("j t p -> j (t p)"))
+            h_turned[s, half] = turned
+
+        def turn_back(s, half):
+            bank = psum.tile([P, 4, P], F32, name="tr", tag="tr")
+            for t in range(4):
+                nc.tensor.transpose(bank[:, t, :], h_turned[s, half][:, P * t : P * (t + 1)], ident[:])
+            nc.scalar.activation(
+                out=h_sb[s][:, BANK * half : BANK * (half + 1)],
+                in_=bank[:].rearrange("p t j -> p (t j)"),
+                func=ACT.Copy,
+                scale=-1.0,
+            )
+
+        def make_h(s):
+            for step in (features, add_terms, turn_back):
+                for half in range(2):
+                    step(s, half)
 
         def put(s, lo, hi):
             nc.vector.tensor_tensor(
@@ -210,11 +249,12 @@ def tile_list_cork_taint_scores_kernel(
                 ALU.mult,
             )
 
-        def pick(s, lo, hi):
-            if lo == 0:
-                x_sb[s] = ringed([P, M], F32, "x", 4)
+        def pick(s, lo, hi, tag):
+            x = ringed([P, hi - lo], F32, tag, 1)
+            for t in range((hi - lo) // P):
+                x_sb[s, lo + P * t] = x[:, P * t : P * (t + 1)]
             nc.vector.tensor_tensor(
-                x_sb[s][:, lo:hi],
+                x[:],
                 pages[s % PAGES][:].indirect(list3[:, lo // 16 : hi // 16]),
                 wgt_sb[:, lo:hi],
                 ALU.mult,
@@ -224,41 +264,49 @@ def tile_list_cork_taint_scores_kernel(
         z_codes = [kept([P, M], U32, "z_c%d" % b) for b in range(2)]
         z_scales = [kept([P, M], U8, "z_s%d" % b) for b in range(2)]
 
-        def add_bark(b, u, k):
-            bank = psum.tile([P, 2, 2, P], F32, name="tr", tag="tr")
-            for t in range(2):
-                cols = slice(CHUNK * k + P * t, CHUNK * k + P * (t + 1))
-                for e in range(2):
-                    nc.tensor.matmul(
-                        bank[:, t, e, :], bark_sb[b, u][:, e, cols], ident[:], start=True, stop=False, is_transpose=True
-                    )
+        def add_bark(b, u, lo, width, tag, bufs):
+            tiles = width // P
+            bank = psum.tile([P, tiles, 2, P], F32, name="tr", tag="tr")
+            places = [(t, e) for e in range(2) for t in range(tiles)]
+            groups = [places] if (b, u) == (1, 1) else [[place] for place in places]
+            for group in groups:
+                for t, e in group:
                     nc.tensor.matmul(
                         bank[:, t, e, :],
-                        x_sb[4 * b + 2 * u + e][:, cols],
+                        bark_sb[b, u][:, e, lo + P * t : lo + P * (t + 1)],
                         ident[:],
-                        start=False,
-                        stop=True,
+                        start=((t, e) == group[0]),
+                        stop=False,
                         is_transpose=True,
                     )
-            turned = ringed([P, 2 * CHUNK], BF16, "z_turned", 8)
-            nc.scalar.copy(
-                turned[:].rearrange("m (t p e) -> m t p e", t=2, e=2), bank[:].rearrange("m t e p -> m t p e")
-            )
-            z_turned[b, u, k] = turned
-
-        def quantize_z(b, k):
-            bank = psum.tile([P, 2, 2, P], F32, name="tr", tag="tr")
-            for t in range(2):
-                for u in range(2):
-                    nc.tensor.transpose(
-                        bank[:, t, u, :], z_turned[b, u, k][:].bitcast(F32)[:, P * t : P * (t + 1)], ident[:]
+                for t, e in group:
+                    nc.tensor.matmul(
+                        bank[:, t, e, :],
+                        x_sb[4 * b + 2 * u + e, lo + P * t],
+                        ident[:],
+                        start=False,
+                        stop=((t, e) == group[-1]),
+                        is_transpose=True,
                     )
-            grouped = ringed([P, 4 * CHUNK], BF16, "z_bf", 4)
+            turned = ringed([P, 2 * width], BF16, tag, bufs)
             nc.scalar.copy(
-                grouped[:].bitcast(F32).rearrange("p (t m u) -> p t m u", t=2, u=2),
+                turned[:].rearrange("m (t p e) -> m t p e", t=tiles, e=2), bank[:].rearrange("m t e p -> m t p e")
+            )
+            for t in range(tiles):
+                z_turned[b, u, lo + P * t] = turned[:].bitcast(F32)[:, P * t : P * (t + 1)]
+
+        def quantize_z(b, lo, width):
+            tiles = width // P
+            bank = psum.tile([P, tiles, 2, P], F32, name="tr", tag="tr")
+            for t in range(tiles):
+                for u in range(2):
+                    nc.tensor.transpose(bank[:, t, u, :], z_turned[b, u, lo + P * t], ident[:])
+            grouped = ringed([P, 4 * width], BF16, "z_bf", 4)
+            nc.scalar.copy(
+                grouped[:].bitcast(F32).rearrange("p (t m u) -> p t m u", t=tiles, u=2),
                 bank[:].rearrange("p t u m -> p t m u"),
             )
-            cols = slice(CHUNK * k, CHUNK * (k + 1))
+            cols = slice(lo, lo + width)
             nc.vector.quantize_mx(out=z_codes[b][:, cols].bitcast(FP8X4), scales=z_scales[b][:, cols], in_=grouped[:])
 
         out_rows = out.rearrange("(p t) m -> p t m", t=4)
@@ -300,11 +348,13 @@ def tile_list_cork_taint_scores_kernel(
         put(0, 0, BANK)
         features(0, 1)
         put(0, BANK, S)
+        make_h(1)
         for s in range(1, 8):
-            features(s, 0)
-            features(s, 1)
             if s < 7:
-                pick(s - 1, 0, M)
+                make_h(s + 1)
+            put(s, 0, S)
+            if s < 7:
+                pick(s - 1, 0, M, "x%d" % ((s - 1) % 4))
             if s == 1:
                 for a in range(2):
                     w1_q[a, 1] = quantize_rows(round_rows(w1_raw[a, 1], nc.scalar.copy), "w1_%d1" % a)
@@ -312,22 +362,17 @@ def tile_list_cork_taint_scores_kernel(
             if s == 4:
                 for b in range(2):
                     w3_q.append(quantize_rows(round_rows(w3_raw[b], nc.scalar.copy), "w3_%d" % b))
-            put(s, 0, S)
-            if s % 2 == 0:
+            if s % 2 == 1 and s > 1:
                 b, u = divmod(s // 2 - 1, 2)
-                for k in range(M // CHUNK):
-                    add_bark(b, u, k)
+                for lo, width in EVEN_CHUNKS:
+                    add_bark(b, u, lo, width, "z_turned", 8)
                     if u == 1:
-                        quantize_z(b, k)
-                if s < 6:
+                        quantize_z(b, lo, width)
+                if b == 0:
                     load_bark(1, u)
-        done = 0
-        for k in range(M // CHUNK):
-            pick(6, CHUNK * k, CHUNK * (k + 1))
-            pick(7, CHUNK * k, CHUNK * (k + 1))
-            add_bark(1, 1, k)
-            quantize_z(1, k)
-            lo, width = Y_CHUNKS[done]
-            if lo + width == CHUNK * (k + 1):
-                scores(lo, width)
-                done = done + 1
+        for k, (lo, width) in enumerate(LAST_CHUNKS):
+            pick(6, lo, lo + width, "x2" if k == 0 else "last%d" % k)
+            pick(7, lo, lo + width, "x7_%d" % k)
+            add_bark(1, 1, lo, width, "last%d" % (k + 2), 1)
+            quantize_z(1, lo, width)
+            scores(lo, width)

@@ -18,10 +18,17 @@ ALU = mybir.AluOpType
 ACT = mybir.ActivationFunctionType
 
 P = 128
+PASS = 512
 BANK = 512
+GROUP = 16
+SLICES = H // P
+LAST = SLICES - 1
 PAGES = 3
-EVEN_CHUNKS = ((0, 256), (256, 256), (512, 256), (768, 256))
+X_SLOTS = 4
+CHUNKS = ((0, 256), (256, 256), (512, 256), (768, 256))
 LAST_CHUNKS = ((0, 128), (128, 256), (384, 256), (640, 256), (896, 128))
+FREE_CHUNKS = 3
+SCORES_BEHIND = 2
 
 
 def tile_list_cork_taint_scores_kernel(
@@ -39,10 +46,13 @@ def tile_list_cork_taint_scores_kernel(
         def ringed(shape, dtype, tag, bufs):
             return ring.tile(shape, dtype, name=tag, tag=tag, bufs=bufs, align_bytes=64)
 
-        list1 = keep.tile([P, S // 16], U16, name="list1")
-        list2 = keep.tile([P, S // 16], U16, name="list2")
-        list3 = keep.tile([P, M // 16], U16, name="list3")
-        tab_s = kept([P, 2 * T], U8, "tab_s")
+        def x_slot(shape, s):
+            return ringed(shape, F32, "x%d" % (s % X_SLOTS), 1)
+
+        list1 = keep.tile([P, S // GROUP], U16, name="list1")
+        list2 = keep.tile([P, S // GROUP], U16, name="list2")
+        list3 = keep.tile([P, M // GROUP], U16, name="list3")
+        tab_s = kept([P, T], U8, "tab_s")
         w2_s_raw = kept([P, 2, H], U8, "w2_s_raw")
         pages = [kept([P, T2], F32, "page%d" % g) for g in range(PAGES)]
         thr_sb = kept([P, 2, 4], F32, "thr_sb")
@@ -50,130 +60,79 @@ def tile_list_cork_taint_scores_kernel(
         wgs_sb = kept([P, S], F32, "wgs_sb")
         wgt_sb = kept([P, M], F32, "wgt_sb")
         ident = kept([P, P], F32, "ident")
-        warm = kept([P, 8], F32, "warm")
+        picked_w = [kept([P, S], U32, "picked_w%d" % a) for a in range(2)]
+        picked_s = [kept([P, S], U8, "picked_s%d" % a) for a in range(2)]
+        z_codes = [kept([P, M], U32, "z_c%d" % b) for b in range(2)]
+        z_scales = [kept([P, M], U8, "z_s%d" % b) for b in range(2)]
 
-        nc.gpsimd.memset(tab_s[:].bitcast(I32), 0)
-        nc.vector.memset(warm[:], 0.0)
-        nc.gpsimd.memset(w2_s_raw[:].rearrange("p a c -> p (a c)").bitcast(I32), 0)
-        nc.scalar.activation(out=warm[:, 4:5], in_=warm[:, 0:1], func=ACT.Tanh)
-
-        def load_w2_words(b):
-            raw = ringed([P, 2, 1024], U8, "w2_raw", 2)
-            nc.sync.dma_start(
-                raw[:].bitcast(I32),
-                w2_words[:, :, 1024 * b : 1024 * (b + 1)].rearrange("a p c -> p a c").bitcast(I32),
-            )
-            return raw
-
-        def load_rows(src):
-            raw = ringed([P, 4, BANK], F32, "w_raw", 3)
-            nc.sync.dma_start(raw[:], src.rearrange("(p j) c -> p j c", j=4))
-            return raw
 
         def load_table_words(a):
-            words = ringed([P, T], I32, "big", 2)
+            words = kept([P, T], I32, "tab_w%d" % a)
             nc.sync.dma_start(words[:], tab_words[a].rearrange("p t i -> p (t i)").bitcast(I32))
             return words
 
-        w1_raw = {}
-        nc.sync.dma_start(list1[:], offs)
-        tab_w = [load_table_words(0)]
-        for q in range(4):
+        def load_w2_words(b):
+            raw = kept([P, 2, 2 * PASS], U8, "w2_raw%d" % b)
             nc.sync.dma_start(
-                tab_s[32 * q : 32 * q + 4, :].bitcast(I32).rearrange("r (a t) -> r a t", a=2),
-                tab_scales[:, 4 * q : 4 * q + 4, :].rearrange("a r t -> r a t").bitcast(I32),
+                raw[:].bitcast(I32),
+                w2_words[:, :, 2 * PASS * b : 2 * PASS * (b + 1)].rearrange("a p c -> p a c").bitcast(I32),
             )
-        for a in range(2):
-            w1_raw[a, 0] = load_rows(w1[512 * a : 512 * (a + 1), 0:512])
-        w2_raw = [load_w2_words(0)]
-        for q in range(4):
-            nc.sync.dma_start(
-                w2_s_raw[32 * q : 32 * q + 4, :, :].bitcast(I32),
-                w2_scales[:, 4 * q : 4 * q + 4, :].rearrange("a r c -> r a c").bitcast(I32),
-            )
-        tab_w.append(load_table_words(1))
-        for g in range(PAGES):
-            (nc.vector, nc.vector, nc.gpsimd)[g].memset(pages[g][:].bitcast(I32), 0)
-        make_identity(nc, ident[:])
-        nc.sync.dma_start(thr_sb[:], thr.rearrange("(b p i) -> p b i", b=2, i=4))
-        nc.sync.dma_start(list2[:], offs2)
-        nc.sync.dma_start(wgs_sb[:], wgs)
-        w2_raw.append(load_w2_words(1))
-        nc.sync.dma_start(list3[:], offs3)
-        nc.sync.dma_start(wgt_sb[:], wgt)
+            return raw
 
-        picked_w = [kept([P, S], U32, "picked_w%d" % a) for a in range(2)]
-        picked_s = [kept([P, S], U8, "picked_s%d" % a) for a in range(2)]
-
-        def pick_words(a, lo, hi):
-            nc.vector.tensor_copy(
-                picked_w[a][:, lo:hi], tab_w[a][:].bitcast(U32).indirect(list1[:, lo // 16 : hi // 16])
-            )
-
-        def deal_w2(b):
-            words = kept([P, 2, 1024], U8, "w2_w%d" % b)
-            scales = kept([P, 2, BANK], U8, "w2_s%d" % b)
-            nc.vector.tensor_copy(
-                words[:].bitcast(U16).rearrange("p a (i q) -> p a i q", i=4),
-                w2_raw[b][:].bitcast(U16).rearrange("p a (q i) -> p a i q", i=4),
-            )
-            nc.vector.tensor_copy(
-                scales[:].rearrange("p a (i q) -> p a i q", i=4),
-                w2_s_raw[:, :, 512 * b : 512 * (b + 1)].rearrange("p a (q i) -> p a i q", i=4),
-            )
-            return words, scales
-
-        def round_rows(raw, copy):
-            grouped = ringed([P, 4 * BANK], BF16, "w_bf", 3)
-            copy(
-                grouped[:].rearrange("p (i q j) -> p q i j", i=4, j=4),
-                raw[:].rearrange("p j (q i) -> p q i j", i=4),
-            )
-            return grouped
-
-        def quantize_rows(grouped, name):
-            codes = kept([P, BANK], U32, name + "_c")
-            scales = kept([P, BANK], U8, name + "_s")
-            nc.vector.quantize_mx(out=codes[:].bitcast(FP8X4), scales=scales[:], in_=grouped[:])
-            return codes, scales
-
-        pick_words(0, 0, S)
-        for a in range(2):
-            nc.vector.tensor_copy(picked_s[a][:], tab_s[:, T * a : T * (a + 1)].indirect(list1[:]))
-        w1_q = {}
-        w1_q[0, 0] = quantize_rows(round_rows(w1_raw[0, 0], nc.scalar.copy), "w1_00")
-        w2_q = [deal_w2(0)]
-        pick_words(1, 0, BANK)
-        w1_q[1, 0] = quantize_rows(round_rows(w1_raw[1, 0], nc.scalar.copy), "w1_10")
-        pick_words(1, BANK, S)
+        def load_pass(rows):
+            raw = ringed([P, 4, PASS], F32, "w_raw", 3)
+            nc.sync.dma_start(raw[:], rows.rearrange("(p j) c -> p j c", j=4))
+            return raw
 
         bark_sb = {}
 
         def load_bark(b, u):
             rows = ringed([P, 2, M], F32, "bark", 2)
             nc.sync.dma_start(
-                rows[:], bark[512 * b : 512 * (b + 1), :].rearrange("(p i) m -> p i m", i=4)[:, 2 * u : 2 * u + 2, :]
+                rows[:],
+                bark[PASS * b : PASS * (b + 1), :].rearrange("(p i) m -> p i m", i=4)[:, 2 * u : 2 * u + 2, :],
             )
             bark_sb[b, u] = rows
 
-        load_bark(0, 0)
-        for a in range(2):
-            w1_raw[a, 1] = load_rows(w1[512 * a : 512 * (a + 1), 512:1024])
-        load_bark(0, 1)
-        w3_raw = [load_rows(w3[512 * b : 512 * (b + 1), :]) for b in range(2)]
-        nc.sync.dma_start(pan_sb[:], pan.rearrange("(p t) -> p t", t=4))
+
+        def pick_words(a, lo, hi):
+            nc.vector.tensor_copy(
+                picked_w[a][:, lo:hi], tab_w[a][:].bitcast(U32).indirect(list1[:, lo // GROUP : hi // GROUP])
+            )
+
+        def deal_w2(b):
+            words = kept([P, 2, 2 * PASS], U8, "w2_w%d" % b)
+            scales = kept([P, 2, PASS], U8, "w2_s%d" % b)
+            nc.vector.tensor_copy(
+                words[:].bitcast(U16).rearrange("p a (i q) -> p a i q", i=4),
+                w2_raw[b][:].bitcast(U16).rearrange("p a (q i) -> p a i q", i=4),
+            )
+            nc.vector.tensor_copy(
+                scales[:].rearrange("p a (i q) -> p a i q", i=4),
+                w2_s_raw[:, :, PASS * b : PASS * (b + 1)].rearrange("p a (q i) -> p a i q", i=4),
+            )
+            return words, scales
+
+        def quantize_pass(raw, name):
+            grouped = ringed([P, 4 * PASS], BF16, "w_bf", 3)
+            nc.scalar.copy(
+                grouped[:].rearrange("p (i q j) -> p q i j", i=4, j=4),
+                raw[:].rearrange("p j (q i) -> p q i j", i=4),
+            )
+            codes = kept([P, PASS], U32, name + "_c")
+            scales = kept([P, PASS], U8, name + "_s")
+            nc.vector.quantize_mx(out=codes[:].bitcast(FP8X4), scales=scales[:], in_=grouped[:])
+            return codes, scales
+
 
         h_sb = {}
-        x_sb = {}
         terms = {}
         h_turned = {}
 
-        def features(s, half):
+        def products(s, half):
             b, i = divmod(s, 4)
             cols = slice(BANK * half, BANK * (half + 1))
             rows = slice(P * i, P * (i + 1))
-            if half == 0:
-                h_sb[s] = ringed([P, S], F32, "h", 3) if s < 7 else ringed([P, S], F32, "x2", 1)
             b_ps = psum.tile([P, BANK], F32, name="mx", tag="mx")
             a_ps = psum.tile([P, BANK], F32, name="mx", tag="mx")
             w2_w, w2_s = w2_q[b]
@@ -199,15 +158,16 @@ def tile_list_cork_taint_scores_kernel(
                 )
             dist = ringed([P, BANK], F32, "dist", 4)
             nc.scalar.activation(out=dist[:], in_=b_ps[:], func=ACT.Abs, bias=thr_sb[:, b, i : i + 1], scale=-1.0)
-            if s == 0:
-                nc.vector.tensor_tensor(h_sb[s][:, cols], a_ps[:], dist[:], ALU.subtract)
+            return a_ps, dist
+
+        def make_terms(s, half):
+            a_ps, dist = products(s, half)
+            if half == 0 and s >= 2:
+                minus_a = x_slot([P, BANK], s - 2)
             else:
-                if half == 0 and s >= 2:
-                    minus_a = ringed([P, BANK], F32, "x%d" % ((s - 2) % 4), 1)
-                else:
-                    minus_a = ringed([P, BANK], F32, "minus_a", 2)
-                nc.scalar.activation(out=minus_a[:], in_=a_ps[:], func=ACT.Copy, scale=-1.0)
-                terms[s, half] = (dist, minus_a)
+                minus_a = ringed([P, BANK], F32, "minus_a", 2)
+            nc.scalar.activation(out=minus_a[:], in_=a_ps[:], func=ACT.Copy, scale=-1.0)
+            terms[s, half] = (dist, minus_a)
 
         def add_terms(s, half):
             bank = psum.tile([P, 4, P], F32, name="tr", tag="tr")
@@ -237,34 +197,36 @@ def tile_list_cork_taint_scores_kernel(
             )
 
         def make_h(s):
-            for step in (features, add_terms, turn_back):
+            h_sb[s] = ringed([P, S], F32, "h", 3) if s < LAST else x_slot([P, S], LAST - 1)
+            for step in (make_terms, add_terms, turn_back):
                 for half in range(2):
                     step(s, half)
 
+
+        x_sb = {}
+
         def put(s, lo, hi):
             nc.vector.tensor_tensor(
-                pages[s % PAGES][:].indirect(list2[:, lo // 16 : hi // 16]),
+                pages[s % PAGES][:].indirect(list2[:, lo // GROUP : hi // GROUP]),
                 h_sb[s][:, lo:hi],
                 wgs_sb[:, lo:hi],
                 ALU.mult,
             )
 
-        def pick(s, lo, hi, tag):
-            x = ringed([P, hi - lo], F32, tag, 1)
-            for t in range((hi - lo) // P):
-                x_sb[s, lo + P * t] = x[:, P * t : P * (t + 1)]
+        def pick(s, lo, hi, x):
             nc.vector.tensor_tensor(
-                x[:],
-                pages[s % PAGES][:].indirect(list3[:, lo // 16 : hi // 16]),
+                x,
+                pages[s % PAGES][:].indirect(list3[:, lo // GROUP : hi // GROUP]),
                 wgt_sb[:, lo:hi],
                 ALU.mult,
             )
+            for t in range((hi - lo) // P):
+                x_sb[s, lo + P * t] = x[:, P * t : P * (t + 1)]
+
 
         z_turned = {}
-        z_codes = [kept([P, M], U32, "z_c%d" % b) for b in range(2)]
-        z_scales = [kept([P, M], U8, "z_s%d" % b) for b in range(2)]
 
-        def add_bark(b, u, lo, width, tag, bufs):
+        def add_bark(b, u, lo, width):
             tiles = width // P
             bank = psum.tile([P, tiles, 2, P], F32, name="tr", tag="tr")
             places = [(t, e) for e in range(2) for t in range(tiles)]
@@ -288,20 +250,19 @@ def tile_list_cork_taint_scores_kernel(
                         stop=((t, e) == group[-1]),
                         is_transpose=True,
                     )
-            turned = ringed([P, 2 * width], BF16, tag, bufs)
+            turned = ringed([P, 2 * width], BF16, "z_turned", 10)
             nc.scalar.copy(
                 turned[:].rearrange("m (t p e) -> m t p e", t=tiles, e=2), bank[:].rearrange("m t e p -> m t p e")
             )
             for t in range(tiles):
                 z_turned[b, u, lo + P * t] = turned[:].bitcast(F32)[:, P * t : P * (t + 1)]
 
-        def quantize_z(b, lo, width):
+        def quantize_z(b, lo, width, grouped):
             tiles = width // P
             bank = psum.tile([P, tiles, 2, P], F32, name="tr", tag="tr")
             for t in range(tiles):
                 for u in range(2):
                     nc.tensor.transpose(bank[:, t, u, :], z_turned[b, u, lo + P * t], ident[:])
-            grouped = ringed([P, 4 * width], BF16, "z_bf", 4)
             nc.scalar.copy(
                 grouped[:].bitcast(F32).rearrange("p (t m u) -> p t m u", t=tiles, u=2),
                 bank[:].rearrange("p t u m -> p t m u"),
@@ -329,13 +290,13 @@ def tile_list_cork_taint_scores_kernel(
                             start=(b == 0),
                             stop=(b == 1),
                         )
-                bent = ringed([P, per_bank, width], F32, "bent", 4)
-                nc.scalar.activation(out=bent[:], in_=y_ps[:], func=ACT.Tanh)
+                tanh_y = ringed([P, per_bank, width], F32, "tanh_y", 4)
+                nc.scalar.activation(out=tanh_y[:], in_=y_ps[:], func=ACT.Tanh)
                 result = ringed([P, per_bank, width], F32, "result", 4)
                 for t in range(per_bank):
                     nc.vector.scalar_tensor_tensor(
                         result[:, t, :],
-                        bent[:, t, :],
+                        tanh_y[:, t, :],
                         pan_sb[:, t0 + t : t0 + t + 1],
                         y_ps[:, t, :],
                         ALU.mult,
@@ -343,36 +304,103 @@ def tile_list_cork_taint_scores_kernel(
                     )
                 nc.sync.dma_start(out_rows[:, t0 : t0 + per_bank, cols], result[:])
 
-        w3_q = []
-        features(0, 0)
-        put(0, 0, BANK)
-        features(0, 1)
-        put(0, BANK, S)
+
+        nc.gpsimd.memset(tab_s[:].bitcast(I32), 0)
+        nc.gpsimd.memset(w2_s_raw[:].rearrange("p a c -> p (a c)").bitcast(I32), 0)
+
+        nc.sync.dma_start(list1[:], offs)
+        tab_w = [load_table_words(0)]
+        for q in range(4):
+            nc.sync.dma_start(
+                tab_s[32 * q : 32 * q + 8, :].bitcast(I32), tab_scales[:, 4 * q : 4 * q + 4, :].bitcast(I32)
+            )
+        w1_raw = {(a, 0): load_pass(w1[PASS * a : PASS * (a + 1), 0:PASS]) for a in range(2)}
+        w2_raw = [load_w2_words(0)]
+        for q in range(4):
+            nc.sync.dma_start(
+                w2_s_raw[32 * q : 32 * q + 4, :, :].bitcast(I32),
+                w2_scales[:, 4 * q : 4 * q + 4, :].rearrange("a r c -> r a c").bitcast(I32),
+            )
+        tab_w.append(load_table_words(1))
+
+        for page in pages:
+            nc.vector.memset(page[:].bitcast(I32), 0)
+        make_identity(nc, ident[:])
+
+        pick_words(0, 0, S)
+        nc.vector.tensor_copy(picked_s[0][:], tab_s[:].indirect(list1[:]))
+        nc.gpsimd.memset(picked_s[1][:].bitcast(I32), 0)
+        for q in range(4):
+            nc.sync.dma_start(
+                picked_s[1][32 * q : 32 * q + 4, :].bitcast(I32), picked_s[0][32 * q + 4 : 32 * q + 8, :].bitcast(I32)
+            )
+        nc.sync.dma_start(thr_sb[:], thr.rearrange("(b p i) -> p b i", b=2, i=4))
+        nc.sync.dma_start(list2[:], offs2)
+        nc.sync.dma_start(wgs_sb[:], wgs)
+        w2_raw.append(load_w2_words(1))
+        nc.sync.dma_start(list3[:], offs3)
+        nc.sync.dma_start(wgt_sb[:], wgt)
+
+        w1_q = {(0, 0): quantize_pass(w1_raw[0, 0], "w1_00")}
+        w2_q = [deal_w2(0)]
+        pick_words(1, 0, BANK)
+        w1_q[1, 0] = quantize_pass(w1_raw[1, 0], "w1_10")
+        pick_words(1, BANK, S)
+
+        load_bark(0, 0)
+        for a in range(2):
+            w1_raw[a, 1] = load_pass(w1[PASS * a : PASS * (a + 1), PASS : 2 * PASS])
+        load_bark(0, 1)
+        w3_raw = [load_pass(w3[PASS * b : PASS * (b + 1), :]) for b in range(2)]
+        nc.sync.dma_start(pan_sb[:], pan.rearrange("(p t) -> p t", t=4))
+
+        h_sb[0] = ringed([P, S], F32, "h", 3)
+        for half in range(2):
+            a_ps, dist = products(0, half)
+            nc.vector.tensor_tensor(h_sb[0][:, BANK * half : BANK * (half + 1)], a_ps[:], dist[:], ALU.subtract)
+            put(0, BANK * half, BANK * (half + 1))
+
+
         make_h(1)
-        for s in range(1, 8):
-            if s < 7:
+        for s in range(1, SLICES):
+            if s < LAST:
                 make_h(s + 1)
             put(s, 0, S)
-            if s < 7:
-                pick(s - 1, 0, M, "x%d" % ((s - 1) % 4))
+            if s < LAST:
+                pick(s - 1, 0, M, x_slot([P, M], s - 1)[:])
             if s == 1:
                 for a in range(2):
-                    w1_q[a, 1] = quantize_rows(round_rows(w1_raw[a, 1], nc.scalar.copy), "w1_%d1" % a)
+                    w1_q[a, 1] = quantize_pass(w1_raw[a, 1], "w1_%d1" % a)
                 w2_q.append(deal_w2(1))
             if s == 4:
-                for b in range(2):
-                    w3_q.append(quantize_rows(round_rows(w3_raw[b], nc.scalar.copy), "w3_%d" % b))
-            if s % 2 == 1 and s > 1:
-                b, u = divmod(s // 2 - 1, 2)
-                for lo, width in EVEN_CHUNKS:
-                    add_bark(b, u, lo, width, "z_turned", 8)
+                w3_q = [quantize_pass(w3_raw[b], "w3_%d" % b) for b in range(2)]
+            if s % 2 == 1 and s >= 3:
+                b, u = divmod((s - 3) // 2, 2)
+                for lo, width in CHUNKS:
+                    add_bark(b, u, lo, width)
                     if u == 1:
-                        quantize_z(b, lo, width)
+                        quantize_z(b, lo, width, ringed([P, 4 * width], BF16, "z_bf", 4))
                 if b == 0:
                     load_bark(1, u)
+
+
+        free_width = LAST_CHUNKS[FREE_CHUNKS][0]
+        x_free = [x_slot([P, free_width], s) for s in (LAST - 1, LAST)]
         for k, (lo, width) in enumerate(LAST_CHUNKS):
-            pick(6, lo, lo + width, "x2" if k == 0 else "last%d" % k)
-            pick(7, lo, lo + width, "x7_%d" % k)
-            add_bark(1, 1, lo, width, "last%d" % (k + 2), 1)
-            quantize_z(1, lo, width)
+            if k < FREE_CHUNKS:
+                xs = [x[:, lo : lo + width] for x in x_free]
+            else:
+                held = ringed([P, 2 * width], F32, "held%d" % (k - FREE_CHUNKS), 1)
+                xs = [held[:, 0:width], held[:, width : 2 * width]]
+            pick(LAST - 1, lo, lo + width, xs[0])
+            pick(LAST, lo, lo + width, xs[1])
+            add_bark(1, 1, lo, width)
+            if k + FREE_CHUNKS < len(LAST_CHUNKS):
+                grouped = ringed([P, 4 * width], BF16, "held%d" % k, 1)
+            else:
+                grouped = ringed([P, 4 * width], BF16, "z_bf", 4)
+            quantize_z(1, lo, width, grouped)
+            if k >= SCORES_BEHIND:
+                scores(*LAST_CHUNKS[k - SCORES_BEHIND])
+        for lo, width in LAST_CHUNKS[-SCORES_BEHIND:]:
             scores(lo, width)

from contextlib import ExitStack

import concourse.mybir as mybir
from concourse.masks import make_identity

K, H, N, T, S, M, T2 = 1024, 1024, 512, 2048, 1024, 1024, 2048
FLOPS = 2 * (2 * K * H * S + H * N * M)

F32 = mybir.dt.float32
BF16 = mybir.dt.bfloat16
I32 = mybir.dt.int32
U32 = mybir.dt.uint32
U16 = mybir.dt.uint16
U8 = mybir.dt.uint8
FP8X4 = mybir.dt.float8_e4m3fn_x4
FP4X4 = mybir.dt.float4_e2m1fn_x4
ALU = mybir.AluOpType
ACT = mybir.ActivationFunctionType

P = 128
PASS = 512
BANK = 512
GROUP = 16
SLICES = H // P
LAST = SLICES - 1
PAGES = 3
X_SLOTS = 4
CHUNKS = ((0, 256), (256, 256), (512, 256), (768, 256))
LAST_CHUNKS = ((0, 128), (128, 256), (384, 256), (640, 256), (896, 128))
FREE_CHUNKS = 3
SCORES_BEHIND = 2


def tile_list_cork_taint_scores_kernel(
    tc, tab_words, tab_scales, offs, offs2, offs3, w1, w2_words, w2_scales, thr, wgs, wgt, bark, w3, pan, out
):
    nc = tc.nc
    with ExitStack() as ctx:
        keep = ctx.enter_context(tc.tile_pool(name="keep", bufs=1))
        ring = ctx.enter_context(tc.tile_pool(name="ring", bufs=2))
        psum = ctx.enter_context(tc.psum_pool(name="psum", bufs=4))

        def kept(shape, dtype, name):
            return keep.tile(shape, dtype, name=name, align_bytes=64)

        def ringed(shape, dtype, tag, bufs):
            return ring.tile(shape, dtype, name=tag, tag=tag, bufs=bufs, align_bytes=64)

        def x_slot(shape, s):
            return ringed(shape, F32, "x%d" % (s % X_SLOTS), 1)

        list1 = keep.tile([P, S // GROUP], U16, name="list1")
        list2 = keep.tile([P, S // GROUP], U16, name="list2")
        list3 = keep.tile([P, M // GROUP], U16, name="list3")
        tab_s = kept([P, T], U8, "tab_s")
        w2_s_raw = kept([P, 2, H], U8, "w2_s_raw")
        pages = [kept([P, T2], F32, "page%d" % g) for g in range(PAGES)]
        thr_sb = kept([P, 2, 4], F32, "thr_sb")
        pan_sb = kept([P, 4], F32, "pan_sb")
        wgs_sb = kept([P, S], F32, "wgs_sb")
        wgt_sb = kept([P, M], F32, "wgt_sb")
        ident = kept([P, P], F32, "ident")
        picked_w = [kept([P, S], U32, "picked_w%d" % a) for a in range(2)]
        picked_s = [kept([P, S], U8, "picked_s%d" % a) for a in range(2)]
        z_codes = [kept([P, M], U32, "z_c%d" % b) for b in range(2)]
        z_scales = [kept([P, M], U8, "z_s%d" % b) for b in range(2)]


        def load_table_words(a):
            words = kept([P, T], I32, "tab_w%d" % a)
            nc.sync.dma_start(words[:], tab_words[a].rearrange("p t i -> p (t i)").bitcast(I32))
            return words

        def load_w2_words(b):
            raw = kept([P, 2, 2 * PASS], U8, "w2_raw%d" % b)
            nc.sync.dma_start(
                raw[:].bitcast(I32),
                w2_words[:, :, 2 * PASS * b : 2 * PASS * (b + 1)].rearrange("a p c -> p a c").bitcast(I32),
            )
            return raw

        def load_pass(rows):
            raw = ringed([P, 4, PASS], F32, "w_raw", 3)
            nc.sync.dma_start(raw[:], rows.rearrange("(p j) c -> p j c", j=4))
            return raw

        bark_sb = {}

        def load_bark(b, u):
            rows = ringed([P, 2, M], F32, "bark", 2)
            nc.sync.dma_start(
                rows[:],
                bark[PASS * b : PASS * (b + 1), :].rearrange("(p i) m -> p i m", i=4)[:, 2 * u : 2 * u + 2, :],
            )
            bark_sb[b, u] = rows


        def pick_words(a, lo, hi):
            nc.vector.tensor_copy(
                picked_w[a][:, lo:hi], tab_w[a][:].bitcast(U32).indirect(list1[:, lo // GROUP : hi // GROUP])
            )

        def deal_w2(b):
            words = kept([P, 2, 2 * PASS], U8, "w2_w%d" % b)
            scales = kept([P, 2, PASS], U8, "w2_s%d" % b)
            nc.vector.tensor_copy(
                words[:].bitcast(U16).rearrange("p a (i q) -> p a i q", i=4),
                w2_raw[b][:].bitcast(U16).rearrange("p a (q i) -> p a i q", i=4),
            )
            nc.vector.tensor_copy(
                scales[:].rearrange("p a (i q) -> p a i q", i=4),
                w2_s_raw[:, :, PASS * b : PASS * (b + 1)].rearrange("p a (q i) -> p a i q", i=4),
            )
            return words, scales

        def quantize_pass(raw, name):
            grouped = ringed([P, 4 * PASS], BF16, "w_bf", 3)
            nc.scalar.copy(
                grouped[:].rearrange("p (i q j) -> p q i j", i=4, j=4),
                raw[:].rearrange("p j (q i) -> p q i j", i=4),
            )
            codes = kept([P, PASS], U32, name + "_c")
            scales = kept([P, PASS], U8, name + "_s")
            nc.vector.quantize_mx(out=codes[:].bitcast(FP8X4), scales=scales[:], in_=grouped[:])
            return codes, scales


        h_sb = {}
        terms = {}
        h_turned = {}

        def products(s, half):
            b, i = divmod(s, 4)
            cols = slice(BANK * half, BANK * (half + 1))
            rows = slice(P * i, P * (i + 1))
            b_ps = psum.tile([P, BANK], F32, name="mx", tag="mx")
            a_ps = psum.tile([P, BANK], F32, name="mx", tag="mx")
            w2_w, w2_s = w2_q[b]
            for a in range(2):
                nc.tensor.matmul_mx(
                    out=b_ps[:],
                    lhsT=w2_w[:, a, 2 * P * i : 2 * P * (i + 1)].bitcast(FP4X4),
                    lhsT_scale=w2_s[:, a, rows],
                    rhs=picked_w[a][:, cols].bitcast(FP8X4),
                    rhs_scale=picked_s[a][:, cols],
                    start=(a == 0),
                    stop=(a == 1),
                )
                codes, scales = w1_q[a, b]
                nc.tensor.matmul_mx(
                    out=a_ps[:],
                    lhsT=codes[:, rows].bitcast(FP8X4),
                    lhsT_scale=scales[:, rows],
                    rhs=picked_w[a][:, cols].bitcast(FP8X4),
                    rhs_scale=picked_s[a][:, cols],
                    start=(a == 0),
                    stop=(a == 1),
                )
            dist = ringed([P, BANK], F32, "dist", 4)
            nc.scalar.activation(out=dist[:], in_=b_ps[:], func=ACT.Abs, bias=thr_sb[:, b, i : i + 1], scale=-1.0)
            return a_ps, dist

        def make_terms(s, half):
            a_ps, dist = products(s, half)
            if half == 0 and s >= 2:
                minus_a = x_slot([P, BANK], s - 2)
            else:
                minus_a = ringed([P, BANK], F32, "minus_a", 2)
            nc.scalar.activation(out=minus_a[:], in_=a_ps[:], func=ACT.Copy, scale=-1.0)
            terms[s, half] = (dist, minus_a)

        def add_terms(s, half):
            bank = psum.tile([P, 4, P], F32, name="tr", tag="tr")
            for t in range(4):
                for n, term in enumerate(terms[s, half]):
                    nc.tensor.matmul(
                        bank[:, t, :],
                        term[:, P * t : P * (t + 1)],
                        ident[:],
                        start=(n == 0),
                        stop=(n == 1),
                        is_transpose=True,
                    )
            turned = ringed([P, BANK], F32, "h_turned", 2)
            nc.scalar.copy(turned[:], bank[:].rearrange("j t p -> j (t p)"))
            h_turned[s, half] = turned

        def turn_back(s, half):
            bank = psum.tile([P, 4, P], F32, name="tr", tag="tr")
            for t in range(4):
                nc.tensor.transpose(bank[:, t, :], h_turned[s, half][:, P * t : P * (t + 1)], ident[:])
            nc.scalar.activation(
                out=h_sb[s][:, BANK * half : BANK * (half + 1)],
                in_=bank[:].rearrange("p t j -> p (t j)"),
                func=ACT.Copy,
                scale=-1.0,
            )

        def make_h(s):
            h_sb[s] = ringed([P, S], F32, "h", 3) if s < LAST else x_slot([P, S], LAST - 1)
            for step in (make_terms, add_terms, turn_back):
                for half in range(2):
                    step(s, half)


        x_sb = {}

        def put(s, lo, hi):
            nc.vector.tensor_tensor(
                pages[s % PAGES][:].indirect(list2[:, lo // GROUP : hi // GROUP]),
                h_sb[s][:, lo:hi],
                wgs_sb[:, lo:hi],
                ALU.mult,
            )

        def pick(s, lo, hi, x):
            nc.vector.tensor_tensor(
                x,
                pages[s % PAGES][:].indirect(list3[:, lo // GROUP : hi // GROUP]),
                wgt_sb[:, lo:hi],
                ALU.mult,
            )
            for t in range((hi - lo) // P):
                x_sb[s, lo + P * t] = x[:, P * t : P * (t + 1)]


        z_turned = {}

        def add_bark(b, u, lo, width):
            tiles = width // P
            bank = psum.tile([P, tiles, 2, P], F32, name="tr", tag="tr")
            places = [(t, e) for e in range(2) for t in range(tiles)]
            groups = [places] if (b, u) == (1, 1) else [[place] for place in places]
            for group in groups:
                for t, e in group:
                    nc.tensor.matmul(
                        bank[:, t, e, :],
                        bark_sb[b, u][:, e, lo + P * t : lo + P * (t + 1)],
                        ident[:],
                        start=((t, e) == group[0]),
                        stop=False,
                        is_transpose=True,
                    )
                for t, e in group:
                    nc.tensor.matmul(
                        bank[:, t, e, :],
                        x_sb[4 * b + 2 * u + e, lo + P * t],
                        ident[:],
                        start=False,
                        stop=((t, e) == group[-1]),
                        is_transpose=True,
                    )
            turned = ringed([P, 2 * width], BF16, "z_turned", 10)
            nc.scalar.copy(
                turned[:].rearrange("m (t p e) -> m t p e", t=tiles, e=2), bank[:].rearrange("m t e p -> m t p e")
            )
            for t in range(tiles):
                z_turned[b, u, lo + P * t] = turned[:].bitcast(F32)[:, P * t : P * (t + 1)]

        def quantize_z(b, lo, width, grouped):
            tiles = width // P
            bank = psum.tile([P, tiles, 2, P], F32, name="tr", tag="tr")
            for t in range(tiles):
                for u in range(2):
                    nc.tensor.transpose(bank[:, t, u, :], z_turned[b, u, lo + P * t], ident[:])
            nc.scalar.copy(
                grouped[:].bitcast(F32).rearrange("p (t m u) -> p t m u", t=tiles, u=2),
                bank[:].rearrange("p t u m -> p t m u"),
            )
            cols = slice(lo, lo + width)
            nc.vector.quantize_mx(out=z_codes[b][:, cols].bitcast(FP8X4), scales=z_scales[b][:, cols], in_=grouped[:])

        out_rows = out.rearrange("(p t) m -> p t m", t=4)

        def scores(lo, width):
            cols = slice(lo, lo + width)
            per_bank = BANK // width
            for t0 in range(0, 4, per_bank):
                y_ps = psum.tile([P, per_bank, width], F32, name="mx", tag="mx")
                for t in range(per_bank):
                    rows = slice(P * (t0 + t), P * (t0 + t + 1))
                    for b in range(2):
                        codes, scales = w3_q[b]
                        nc.tensor.matmul_mx(
                            out=y_ps[:, t, :],
                            lhsT=codes[:, rows].bitcast(FP8X4),
                            lhsT_scale=scales[:, rows],
                            rhs=z_codes[b][:, cols].bitcast(FP8X4),
                            rhs_scale=z_scales[b][:, cols],
                            start=(b == 0),
                            stop=(b == 1),
                        )
                tanh_y = ringed([P, per_bank, width], F32, "tanh_y", 4)
                nc.scalar.activation(out=tanh_y[:], in_=y_ps[:], func=ACT.Tanh)
                result = ringed([P, per_bank, width], F32, "result", 4)
                for t in range(per_bank):
                    nc.vector.scalar_tensor_tensor(
                        result[:, t, :],
                        tanh_y[:, t, :],
                        pan_sb[:, t0 + t : t0 + t + 1],
                        y_ps[:, t, :],
                        ALU.mult,
                        ALU.add,
                    )
                nc.sync.dma_start(out_rows[:, t0 : t0 + per_bank, cols], result[:])


        nc.gpsimd.memset(tab_s[:].bitcast(I32), 0)
        nc.gpsimd.memset(w2_s_raw[:].rearrange("p a c -> p (a c)").bitcast(I32), 0)

        nc.sync.dma_start(list1[:], offs)
        tab_w = [load_table_words(0)]
        for q in range(4):
            nc.sync.dma_start(
                tab_s[32 * q : 32 * q + 8, :].bitcast(I32), tab_scales[:, 4 * q : 4 * q + 4, :].bitcast(I32)
            )
        w1_raw = {(a, 0): load_pass(w1[PASS * a : PASS * (a + 1), 0:PASS]) for a in range(2)}
        w2_raw = [load_w2_words(0)]
        for q in range(4):
            nc.sync.dma_start(
                w2_s_raw[32 * q : 32 * q + 4, :, :].bitcast(I32),
                w2_scales[:, 4 * q : 4 * q + 4, :].rearrange("a r c -> r a c").bitcast(I32),
            )
        tab_w.append(load_table_words(1))

        for page in pages:
            nc.vector.memset(page[:].bitcast(I32), 0)
        make_identity(nc, ident[:])

        pick_words(0, 0, S)
        nc.vector.tensor_copy(picked_s[0][:], tab_s[:].indirect(list1[:]))
        nc.gpsimd.memset(picked_s[1][:].bitcast(I32), 0)
        for q in range(4):
            nc.sync.dma_start(
                picked_s[1][32 * q : 32 * q + 4, :].bitcast(I32), picked_s[0][32 * q + 4 : 32 * q + 8, :].bitcast(I32)
            )
        nc.sync.dma_start(thr_sb[:], thr.rearrange("(b p i) -> p b i", b=2, i=4))
        nc.sync.dma_start(list2[:], offs2)
        nc.sync.dma_start(wgs_sb[:], wgs)
        w2_raw.append(load_w2_words(1))
        nc.sync.dma_start(list3[:], offs3)
        nc.sync.dma_start(wgt_sb[:], wgt)

        w1_q = {(0, 0): quantize_pass(w1_raw[0, 0], "w1_00")}
        w2_q = [deal_w2(0)]
        pick_words(1, 0, BANK)
        w1_q[1, 0] = quantize_pass(w1_raw[1, 0], "w1_10")
        pick_words(1, BANK, S)

        load_bark(0, 0)
        for a in range(2):
            w1_raw[a, 1] = load_pass(w1[PASS * a : PASS * (a + 1), PASS : 2 * PASS])
        load_bark(0, 1)
        w3_raw = [load_pass(w3[PASS * b : PASS * (b + 1), :]) for b in range(2)]
        nc.sync.dma_start(pan_sb[:], pan.rearrange("(p t) -> p t", t=4))

        h_sb[0] = ringed([P, S], F32, "h", 3)
        for half in range(2):
            a_ps, dist = products(0, half)
            nc.vector.tensor_tensor(h_sb[0][:, BANK * half : BANK * (half + 1)], a_ps[:], dist[:], ALU.subtract)
            put(0, BANK * half, BANK * (half + 1))


        make_h(1)
        for s in range(1, SLICES):
            if s < LAST:
                make_h(s + 1)
            put(s, 0, S)
            if s < LAST:
                pick(s - 1, 0, M, x_slot([P, M], s - 1)[:])
            if s == 1:
                for a in range(2):
                    w1_q[a, 1] = quantize_pass(w1_raw[a, 1], "w1_%d1" % a)
                w2_q.append(deal_w2(1))
            if s == 4:
                w3_q = [quantize_pass(w3_raw[b], "w3_%d" % b) for b in range(2)]
            if s % 2 == 1 and s >= 3:
                b, u = divmod((s - 3) // 2, 2)
                for lo, width in CHUNKS:
                    add_bark(b, u, lo, width)
                    if u == 1:
                        quantize_z(b, lo, width, ringed([P, 4 * width], BF16, "z_bf", 4))
                if b == 0:
                    load_bark(1, u)


        free_width = LAST_CHUNKS[FREE_CHUNKS][0]
        x_free = [x_slot([P, free_width], s) for s in (LAST - 1, LAST)]
        for k, (lo, width) in enumerate(LAST_CHUNKS):
            if k < FREE_CHUNKS:
                xs = [x[:, lo : lo + width] for x in x_free]
            else:
                held = ringed([P, 2 * width], F32, "held%d" % (k - FREE_CHUNKS), 1)
                xs = [held[:, 0:width], held[:, width : 2 * width]]
            pick(LAST - 1, lo, lo + width, xs[0])
            pick(LAST, lo, lo + width, xs[1])
            add_bark(1, 1, lo, width)
            if k + FREE_CHUNKS < len(LAST_CHUNKS):
                grouped = ringed([P, 4 * width], BF16, "held%d" % k, 1)
            else:
                grouped = ringed([P, 4 * width], BF16, "z_bf", 4)
            quantize_z(1, lo, width, grouped)
            if k >= SCORES_BEHIND:
                scores(*LAST_CHUNKS[k - SCORES_BEHIND])
        for lo, width in LAST_CHUNKS[-SCORES_BEHIND:]:
            scores(lo, width)
